import numpy as np
import ml_dtypes


def mxq(x, axis, fmt="e4m3"):
    dtype, down = {"e4m3": (ml_dtypes.float8_e4m3fn, 7), "e5m2": (ml_dtypes.float8_e5m2, 14)}[fmt]
    v = np.moveaxis(np.asarray(x, np.float32).astype(ml_dtypes.bfloat16).astype(np.float64), axis, -1)
    blocks = v.reshape(v.shape[:-1] + (-1, 32))
    amax = np.abs(blocks).max(-1, keepdims=True)
    byte = np.maximum(np.where(amax > 0, np.frexp(amax)[1] - 1 + 127, 0) - down, 1)
    scale = np.exp2(byte - 127.0)
    codes = (blocks / scale).astype(np.float32).astype(dtype).astype(np.float64)
    return np.moveaxis((codes * scale).reshape(v.shape), -1, axis)


WIDE = False


def mx_kscale(k):
    if not WIDE:
        return np.ones(k)
    levels = np.array([10, -10, 5, -5, 0])
    if k % 512:
        return np.exp2(np.random.permutation(np.resize(levels, k // 32))).repeat(32)
    a = np.empty((k // 512, 16))
    for p in range(k // 512):
        a[p, :8] = np.random.permutation(np.resize(levels, 8))
        for g in range(8):
            far = levels[np.abs(levels - a[p, g]) >= 10]
            a[p, g + 8] = far[np.random.randint(len(far))]
    return np.exp2(a.ravel()).repeat(32)


def f64(x):
    return np.asarray(x).astype(np.float64)


def striped(idx):
    return np.tile(idx.reshape(-1, 16).T, (8, 1)).astype(np.uint16)


def unstriped(offs):
    return offs[:16].T.reshape(-1).astype(np.int64)


def pack_weight(w):
    k, n = w.shape
    w = f64(np.asarray(w, np.float32).astype(ml_dtypes.bfloat16)).reshape(k // 32, 32, n)
    amax = np.abs(w).max(1)
    byte = np.clip(np.where(amax > 0, np.frexp(amax)[1] - 1 + 127 - 7, 1), 1, 254)
    scaled = (w * np.exp2(127.0 - byte)[:, None, :]).reshape(k, n).astype(np.float32)
    words = np.ascontiguousarray(scaled.reshape(k // 512, 128, 4, n).transpose(0, 1, 3, 2)).astype(ml_dtypes.float8_e4m3fn).view(np.uint8)
    return words, np.ascontiguousarray(byte.astype(np.uint8).reshape(k // 512, 16, n))


def unpack_weight(words, scales):
    g, p, n, _ = words.shape
    vals = np.ascontiguousarray(words).view(ml_dtypes.float8_e4m3fn).astype(np.float64) * np.repeat(np.exp2(scales.astype(np.float64) - 127.0), 8, axis=1)[..., None]
    return vals.transpose(0, 1, 3, 2).reshape(g * 512, n)


K, T, S, J = 512, 2048, 512, 256


def setup_inputs():
    n = np.random.standard_normal
    s = mx_kscale(K)[:, None]
    part = np.random.uniform(0.2, 0.8, (J, 1))
    packed_xT = pack_weight(n((K, T)) * s)
    return {
        "x_words": packed_xT[0],
        "x_scales": packed_xT[1],
        "hT": (n((K, J)) / np.sqrt(K) / s).astype(np.float32),
        "near": (np.random.dirichlet(np.ones(S), J)).astype(np.float32),
        "mix": (np.concatenate([part, 1.0 - part], axis=1)).astype(np.float32),
        "offs": striped(np.random.permutation(T)[:S]),
    }


def reference(x_words, x_scales, hT, near, mix, offs):
    hTq = mxq(f64(hT), 0, "e4m3")
    xq = unpack_weight(x_words, x_scales)[:, unstriped(offs)]
    y = hTq.T @ xq
    e = np.exp(y - y.max(axis=1, keepdims=True))
    p = e / e.sum(axis=1, keepdims=True)
    return np.maximum(f64(mix)[:, 0:1] * p, f64(mix)[:, 1:2] * f64(near))

@@ -1,0 +1,99 @@
+from contextlib import ExitStack
+
+import concourse.mybir as mybir
+
+K, T, S, J = 512, 2048, 512, 256
+FLOPS = 2 * K * S * J
+
+F32 = mybir.dt.float32
+BF16 = mybir.dt.bfloat16
+I32 = mybir.dt.int32
+U32 = mybir.dt.uint32
+U16 = mybir.dt.uint16
+U8 = mybir.dt.uint8
+FP8X4 = mybir.dt.float8_e4m3fn_x4
+ALU = mybir.AluOpType
+ACT = mybir.ActivationFunctionType
+AX = mybir.AxisListType
+
+P = 128
+PACK = 4
+TILES = J // P
+HALF = S // 2
+
+
+def tile_picked_zknn_max_p_kernel(tc, x_words, x_scales, hT, near, mix, offs, out):
+    nc = tc.nc
+    with ExitStack() as ctx:
+        sb = ctx.enter_context(tc.tile_pool(name="sb", bufs=1))
+        ps = ctx.enter_context(tc.psum_pool(name="ps", bufs=1))
+
+        offsets = sb.tile([P, S // 16], U16, name="offsets")
+        h_raw = sb.tile([P, PACK, J], F32, name="h_raw")
+        scale_table = sb.tile([P, T], U8, name="scale_table", align_bytes=64)
+        word_table = sb.tile([P, T], I32, name="word_table", align_bytes=64)
+        mix_sb = sb.tile([P, TILES, 2], F32, name="mix_sb")
+        near_sb = sb.tile([P, TILES, S], F32, name="near_sb")
+        warm = sb.tile([P, 1], F32, name="warm")
+        warm_out = sb.tile([P, 1], F32, name="warm_out")
+
+        nc.vector.memset(scale_table[:].bitcast(I32), 0)
+        nc.gpsimd.memset(warm[:], 0.0)
+        nc.scalar.activation(warm_out[:], warm[:], ACT.Exp)
+
+        nc.sync.dma_start(offsets[:], offs)
+        nc.sync.dma_start(h_raw[:], hT.rearrange("(p j) w -> p j w", j=PACK))
+        for q in range(4):
+            nc.sync.dma_start(scale_table[32 * q : 32 * q + 4, :].bitcast(I32), x_scales[0, 4 * q : 4 * q + 4, :].bitcast(I32))
+        nc.sync.dma_start(word_table[:], x_words[0].rearrange("p c r -> p (c r)").bitcast(I32))
+        with nc.allow_non_contiguous_dma(reason="two floats a position"):
+            nc.sync.dma_start(mix_sb[:], mix.rearrange("(i p) c -> p i c", p=P))
+        nc.sync.dma_start(near_sb[:], near.rearrange("(i p) s -> p i s", p=P))
+
+        x_sc = sb.tile([P, S], U8, name="x_sc", align_bytes=64)
+        nc.vector.tensor_copy(x_sc[:], scale_table[:].indirect(offsets[:]))
+
+        h_codes, h_sc = [], []
+        for i in range(TILES):
+            grouped = sb.tile([P, P, PACK], BF16, name="grouped%d" % i, align_bytes=64)
+            nc.scalar.copy(grouped[:], h_raw[:, :, i * P : (i + 1) * P].rearrange("p j w -> p w j"))
+            codes = sb.tile([P, P], U32, name="h_codes%d" % i, align_bytes=64)
+            sc = sb.tile([P, P], U8, name="h_sc%d" % i, align_bytes=64)
+            nc.vector.quantize_mx(out=codes[:].bitcast(FP8X4), scales=sc[:], in_=grouped[:].rearrange("p w j -> p (w j)"))
+            h_codes.append(codes)
+            h_sc.append(sc)
+
+        acc = [ps.tile([P, S], F32, name="acc%d" % i) for i in range(TILES)]
+        for u in range(2):
+            words = sb.tile([P, HALF], U32, name="x_codes%d" % u, align_bytes=64)
+            nc.vector.tensor_copy(words[:], word_table[:].bitcast(U32).indirect(offsets[:, u * 16 : (u + 1) * 16]))
+            for i in range(TILES):
+                nc.tensor.matmul_mx(
+                    out=acc[i][:, u * HALF : (u + 1) * HALF],
+                    lhsT=h_codes[i][:].bitcast(FP8X4),
+                    lhsT_scale=h_sc[i][:],
+                    rhs=words[:].bitcast(FP8X4),
+                    rhs_scale=x_sc[:, u * HALF : (u + 1) * HALF],
+                    start=True,
+                    stop=True,
+                )
+
+        weighted = []
+        for i in range(TILES):
+            w = sb.tile([P, S], F32, name="weighted%d" % i)
+            nc.scalar.activation(w[:], near_sb[:, i, :], ACT.Copy, scale=mix_sb[:, i, 1:2])
+            weighted.append(w)
+
+        for i in range(TILES):
+            neg_max = sb.tile([P, 1], F32, name="neg_max%d" % i)
+            nc.vector.tensor_reduce(neg_max[:], acc[i][:], AX.X, ALU.max, negate=True)
+            e = sb.tile([P, S], F32, name="e%d" % i)
+            total = sb.tile([P, 1], F32, name="total%d" % i)
+            nc.scalar.activation(e[:], acc[i][:], ACT.Exp, bias=neg_max[:], scale=1.0, accum_out=total[:])
+            recip = sb.tile([P, 1], F32, name="recip%d" % i)
+            nc.vector.reciprocal(recip[:], total[:])
+            factor = sb.tile([P, 1], F32, name="factor%d" % i)
+            nc.vector.tensor_tensor(factor[:], recip[:], mix_sb[:, i, 0:1], ALU.mult)
+            res = sb.tile([P, S], F32, name="res%d" % i)
+            nc.vector.scalar_tensor_tensor(res[:], e[:], factor[:], weighted[i][:], ALU.mult, ALU.max)
+            nc.sync.dma_start(out[i * P : (i + 1) * P, :], res[:])

@@ -20,6 +20,7 @@ P = 128
 PACK = 4
 TILES = J // P
 HALF = S // 2
+BIG = 1e38
 
 
 def tile_picked_zknn_max_p_kernel(tc, x_words, x_scales, hT, near, mix, offs, out):
@@ -63,13 +64,13 @@ def tile_picked_zknn_max_p_kernel(tc, x_words, x_scales, hT, near, mix, offs, ou
             h_codes.append(codes)
             h_sc.append(sc)
 
-        acc = [ps.tile([P, S], F32, name="acc%d" % i) for i in range(TILES)]
+        acc = [[ps.tile([P, HALF], F32, name="acc%d_%d" % (i, u)) for u in range(2)] for i in range(TILES)]
         for u in range(2):
             words = sb.tile([P, HALF], U32, name="x_codes%d" % u, align_bytes=64)
             nc.vector.tensor_copy(words[:], word_table[:].bitcast(U32).indirect(offsets[:, u * 16 : (u + 1) * 16]))
             for i in range(TILES):
                 nc.tensor.matmul_mx(
-                    out=acc[i][:, u * HALF : (u + 1) * HALF],
+                    out=acc[i][u][:],
                     lhsT=h_codes[i][:].bitcast(FP8X4),
                     lhsT_scale=h_sc[i][:],
                     rhs=words[:].bitcast(FP8X4),
@@ -81,19 +82,44 @@ def tile_picked_zknn_max_p_kernel(tc, x_words, x_scales, hT, near, mix, offs, ou
         weighted = []
         for i in range(TILES):
             w = sb.tile([P, S], F32, name="weighted%d" % i)
-            nc.scalar.activation(w[:], near_sb[:, i, :], ACT.Copy, scale=mix_sb[:, i, 1:2])
+            nc.gpsimd.tensor_scalar(w[:], near_sb[:, i, :], mix_sb[:, i, 1:2], 0.0, ALU.mult, ALU.add)
             weighted.append(w)
 
+        inv_raw = sb.tile([P, TILES], F32, name="inv_raw")
+        nc.vector.reciprocal(inv_raw[:], mix_sb[:, :, 0])
+        inv_mix = sb.tile([P, TILES], F32, name="inv_mix")
+        nc.vector.tensor_scalar(inv_mix[:], inv_raw[:], BIG, -BIG, ALU.min, ALU.max)
+
+        neg_max = [sb.tile([P, 2], F32, name="neg_max%d" % i) for i in range(TILES)]
+        sums = [sb.tile([P, 2], F32, name="sums%d" % i) for i in range(TILES)]
+        es = [sb.tile([P, S], F32, name="e%d" % i) for i in range(TILES)]
         for i in range(TILES):
-            neg_max = sb.tile([P, 1], F32, name="neg_max%d" % i)
-            nc.vector.tensor_reduce(neg_max[:], acc[i][:], AX.X, ALU.max, negate=True)
-            e = sb.tile([P, S], F32, name="e%d" % i)
+            nc.vector.tensor_reduce(neg_max[i][:, 0:1], acc[i][0][:], AX.X, ALU.max, negate=True)
+            nc.scalar.activation(es[i][:, :HALF], acc[i][0][:], ACT.Exp, bias=neg_max[i][:, 0:1], scale=1.0, accum_out=sums[i][:, 0:1])
+        shifts = []
+        for i in range(TILES):
+            neg_y = sb.tile([P, HALF], F32, name="neg_y%d" % i)
+            nc.vector.tensor_scalar(neg_y[:], acc[i][1][:], -1.0, neg_max[i][:, 0:1], ALU.mult, ALU.min, accum_out=neg_max[i][:, 1:2])
+            shift = sb.tile([P, 1], F32, name="shift%d" % i)
+            nc.scalar.activation(shift[:], neg_max[i][:, 0:1], ACT.Exp, bias=neg_max[i][:, 1:2], scale=-1.0)
+            nc.scalar.activation(es[i][:, HALF:], neg_y[:], ACT.Exp, bias=neg_max[i][:, 1:2], scale=-1.0, accum_out=sums[i][:, 1:2])
+            shifts.append(shift)
+        factors = []
+        for i in range(TILES):
+            inv = inv_mix[:, i : i + 1]
+            part = sb.tile([P, 1], F32, name="part%d" % i)
+            nc.vector.tensor_scalar(part[:], sums[i][:, 0:1], shifts[i][:], inv, ALU.mult, ALU.mult)
             total = sb.tile([P, 1], F32, name="total%d" % i)
-            nc.scalar.activation(e[:], acc[i][:], ACT.Exp, bias=neg_max[:], scale=1.0, accum_out=total[:])
-            recip = sb.tile([P, 1], F32, name="recip%d" % i)
-            nc.vector.reciprocal(recip[:], total[:])
-            factor = sb.tile([P, 1], F32, name="factor%d" % i)
-            nc.vector.tensor_tensor(factor[:], recip[:], mix_sb[:, i, 0:1], ALU.mult)
-            res = sb.tile([P, S], F32, name="res%d" % i)
-            nc.vector.scalar_tensor_tensor(res[:], e[:], factor[:], weighted[i][:], ALU.mult, ALU.max)
-            nc.sync.dma_start(out[i * P : (i + 1) * P, :], res[:])
+            nc.vector.tensor_scalar(total[:], sums[i][:, 1:2], inv, part[:], ALU.mult, ALU.add)
+            second = sb.tile([P, 1], F32, name="second%d" % i)
+            nc.vector.reciprocal(second[:], total[:])
+            first = sb.tile([P, 1], F32, name="first%d" % i)
+            nc.vector.tensor_tensor(first[:], second[:], shifts[i][:], ALU.mult)
+            factors.append((first, second))
+        pieces = [(0, 256, 512), (0, 0, 256), (1, 256, 512), (1, 0, 128), (1, 128, 256)]
+        for n, (i, c0, c1) in enumerate(pieces):
+            u = c0 // HALF
+            res = sb.tile([P, c1 - c0], F32, name="res%d" % n)
+            nc.vector.scalar_tensor_tensor(res[:], es[i][:, c0:c1], factors[i][u][:], weighted[i][:, c0:c1], ALU.mult, ALU.max)
+            queue = nc.sync if n % 2 == 0 else nc.scalar
+            queue.dma_start(out[i * P : (i + 1) * P, c0:c1], res[:])

@@ -42,10 +42,10 @@ def tile_picked_zknn_max_p_kernel(tc, x_words, x_scales, hT, near, mix, offs, ou
         nc.gpsimd.memset(warm[:], 0.0)
         nc.scalar.activation(warm_out[:], warm[:], ACT.Exp)
 
-        nc.sync.dma_start(offsets[:], offs)
         nc.sync.dma_start(h_raw[:], hT.rearrange("(p j) w -> p j w", j=PACK))
-        for q in range(4):
-            nc.sync.dma_start(scale_table[32 * q : 32 * q + 4, :].bitcast(I32), x_scales[0, 4 * q : 4 * q + 4, :].bitcast(I32))
+        nc.sync.dma_start(offsets[:], offs)
+        for r in range(4):
+            nc.sync.dma_start(scale_table[r:P:32, :].bitcast(I32), x_scales[0, r:16:4, :].bitcast(I32))
         nc.sync.dma_start(word_table[:], x_words[0].rearrange("p c r -> p (c r)").bitcast(I32))
         with nc.allow_non_contiguous_dma(reason="two floats a position"):
             nc.sync.dma_start(mix_sb[:], mix.rearrange("(i p) c -> p i c", p=P))
@@ -57,7 +57,8 @@ def tile_picked_zknn_max_p_kernel(tc, x_words, x_scales, hT, near, mix, offs, ou
         h_codes, h_sc = [], []
         for i in range(TILES):
             grouped = sb.tile([P, P, PACK], BF16, name="grouped%d" % i, align_bytes=64)
-            nc.scalar.copy(grouped[:], h_raw[:, :, i * P : (i + 1) * P].rearrange("p j w -> p w j"))
+            cast = nc.vector.tensor_copy if i == 0 else nc.scalar.copy
+            cast(grouped[:], h_raw[:, :, i * P : (i + 1) * P].rearrange("p j w -> p w j"))
             codes = sb.tile([P, P], U32, name="h_codes%d" % i, align_bytes=64)
             sc = sb.tile([P, P], U8, name="h_sc%d" % i, align_bytes=64)
             nc.vector.quantize_mx(out=codes[:].bitcast(FP8X4), scales=sc[:], in_=grouped[:].rearrange("p w j -> p (w j)"))
@@ -116,7 +117,7 @@ def tile_picked_zknn_max_p_kernel(tc, x_words, x_scales, hT, near, mix, offs, ou
             first = sb.tile([P, 1], F32, name="first%d" % i)
             nc.vector.tensor_tensor(first[:], second[:], shifts[i][:], ALU.mult)
             factors.append((first, second))
-        pieces = [(0, 256, 512), (0, 0, 256), (1, 256, 512), (1, 0, 128), (1, 128, 256)]
+        pieces = [(0, 256, 384), (0, 384, 512), (0, 0, 256), (1, 256, 512), (1, 0, 128), (1, 128, 256)]
         for n, (i, c0, c1) in enumerate(pieces):
             u = c0 // HALF
             res = sb.tile([P, c1 - c0], F32, name="res%d" % n)

@@ -89,7 +89,7 @@ def tile_picked_zknn_max_p_kernel(tc, x_words, x_scales, hT, near, mix, offs, ou
         inv_raw = sb.tile([P, TILES], F32, name="inv_raw")
         nc.vector.reciprocal(inv_raw[:], mix_sb[:, :, 0])
         inv_mix = sb.tile([P, TILES], F32, name="inv_mix")
-        nc.vector.tensor_scalar(inv_mix[:], inv_raw[:], BIG, -BIG, ALU.min, ALU.max)
+        nc.gpsimd.tensor_scalar(inv_mix[:], inv_raw[:], BIG, -BIG, ALU.min, ALU.max)
 
         neg_max = [sb.tile([P, 2], F32, name="neg_max%d" % i) for i in range(TILES)]
         sums = [sb.tile([P, 2], F32, name="sums%d" % i) for i in range(TILES)]

from contextlib import ExitStack

import concourse.mybir as mybir

K, T, S, J = 512, 2048, 512, 256
FLOPS = 2 * K * S * J

F32 = mybir.dt.float32
BF16 = mybir.dt.bfloat16
I32 = mybir.dt.int32
U32 = mybir.dt.uint32
U16 = mybir.dt.uint16
U8 = mybir.dt.uint8
FP8X4 = mybir.dt.float8_e4m3fn_x4
ALU = mybir.AluOpType
ACT = mybir.ActivationFunctionType
AX = mybir.AxisListType

P = 128
PACK = 4
TILES = J // P
HALF = S // 2
BIG = 1e38


def tile_picked_zknn_max_p_kernel(tc, x_words, x_scales, hT, near, mix, offs, out):
    nc = tc.nc
    with ExitStack() as ctx:
        sb = ctx.enter_context(tc.tile_pool(name="sb", bufs=1))
        ps = ctx.enter_context(tc.psum_pool(name="ps", bufs=1))

        offsets = sb.tile([P, S // 16], U16, name="offsets")
        h_raw = sb.tile([P, PACK, J], F32, name="h_raw")
        scale_table = sb.tile([P, T], U8, name="scale_table", align_bytes=64)
        word_table = sb.tile([P, T], I32, name="word_table", align_bytes=64)
        mix_sb = sb.tile([P, TILES, 2], F32, name="mix_sb")
        near_sb = sb.tile([P, TILES, S], F32, name="near_sb")
        warm = sb.tile([P, 1], F32, name="warm")
        warm_out = sb.tile([P, 1], F32, name="warm_out")

        nc.vector.memset(scale_table[:].bitcast(I32), 0)
        nc.gpsimd.memset(warm[:], 0.0)
        nc.scalar.activation(warm_out[:], warm[:], ACT.Exp)

        nc.sync.dma_start(h_raw[:], hT.rearrange("(p j) w -> p j w", j=PACK))
        nc.sync.dma_start(offsets[:], offs)
        for r in range(4):
            nc.sync.dma_start(scale_table[r:P:32, :].bitcast(I32), x_scales[0, r:16:4, :].bitcast(I32))
        nc.sync.dma_start(word_table[:], x_words[0].rearrange("p c r -> p (c r)").bitcast(I32))
        with nc.allow_non_contiguous_dma(reason="two floats a position"):
            nc.sync.dma_start(mix_sb[:], mix.rearrange("(i p) c -> p i c", p=P))
        nc.sync.dma_start(near_sb[:], near.rearrange("(i p) s -> p i s", p=P))

        x_sc = sb.tile([P, S], U8, name="x_sc", align_bytes=64)
        nc.vector.tensor_copy(x_sc[:], scale_table[:].indirect(offsets[:]))

        h_codes, h_sc = [], []
        for i in range(TILES):
            grouped = sb.tile([P, P, PACK], BF16, name="grouped%d" % i, align_bytes=64)
            cast = nc.vector.tensor_copy if i == 0 else nc.scalar.copy
            cast(grouped[:], h_raw[:, :, i * P : (i + 1) * P].rearrange("p j w -> p w j"))
            codes = sb.tile([P, P], U32, name="h_codes%d" % i, align_bytes=64)
            sc = sb.tile([P, P], U8, name="h_sc%d" % i, align_bytes=64)
            nc.vector.quantize_mx(out=codes[:].bitcast(FP8X4), scales=sc[:], in_=grouped[:].rearrange("p w j -> p (w j)"))
            h_codes.append(codes)
            h_sc.append(sc)

        acc = [[ps.tile([P, HALF], F32, name="acc%d_%d" % (i, u)) for u in range(2)] for i in range(TILES)]
        for u in range(2):
            words = sb.tile([P, HALF], U32, name="x_codes%d" % u, align_bytes=64)
            nc.vector.tensor_copy(words[:], word_table[:].bitcast(U32).indirect(offsets[:, u * 16 : (u + 1) * 16]))
            for i in range(TILES):
                nc.tensor.matmul_mx(
                    out=acc[i][u][:],
                    lhsT=h_codes[i][:].bitcast(FP8X4),
                    lhsT_scale=h_sc[i][:],
                    rhs=words[:].bitcast(FP8X4),
                    rhs_scale=x_sc[:, u * HALF : (u + 1) * HALF],
                    start=True,
                    stop=True,
                )

        weighted = []
        for i in range(TILES):
            w = sb.tile([P, S], F32, name="weighted%d" % i)
            nc.gpsimd.tensor_scalar(w[:], near_sb[:, i, :], mix_sb[:, i, 1:2], 0.0, ALU.mult, ALU.add)
            weighted.append(w)

        inv_raw = sb.tile([P, TILES], F32, name="inv_raw")
        nc.vector.reciprocal(inv_raw[:], mix_sb[:, :, 0])
        inv_mix = sb.tile([P, TILES], F32, name="inv_mix")
        nc.gpsimd.tensor_scalar(inv_mix[:], inv_raw[:], BIG, -BIG, ALU.min, ALU.max)

        neg_max = [sb.tile([P, 2], F32, name="neg_max%d" % i) for i in range(TILES)]
        sums = [sb.tile([P, 2], F32, name="sums%d" % i) for i in range(TILES)]
        es = [sb.tile([P, S], F32, name="e%d" % i) for i in range(TILES)]
        for i in range(TILES):
            nc.vector.tensor_reduce(neg_max[i][:, 0:1], acc[i][0][:], AX.X, ALU.max, negate=True)
            nc.scalar.activation(es[i][:, :HALF], acc[i][0][:], ACT.Exp, bias=neg_max[i][:, 0:1], scale=1.0, accum_out=sums[i][:, 0:1])
        shifts = []
        for i in range(TILES):
            neg_y = sb.tile([P, HALF], F32, name="neg_y%d" % i)
            nc.vector.tensor_scalar(neg_y[:], acc[i][1][:], -1.0, neg_max[i][:, 0:1], ALU.mult, ALU.min, accum_out=neg_max[i][:, 1:2])
            shift = sb.tile([P, 1], F32, name="shift%d" % i)
            nc.scalar.activation(shift[:], neg_max[i][:, 0:1], ACT.Exp, bias=neg_max[i][:, 1:2], scale=-1.0)
            nc.scalar.activation(es[i][:, HALF:], neg_y[:], ACT.Exp, bias=neg_max[i][:, 1:2], scale=-1.0, accum_out=sums[i][:, 1:2])
            shifts.append(shift)
        factors = []
        for i in range(TILES):
            inv = inv_mix[:, i : i + 1]
            part = sb.tile([P, 1], F32, name="part%d" % i)
            nc.vector.tensor_scalar(part[:], sums[i][:, 0:1], shifts[i][:], inv, ALU.mult, ALU.mult)
            total = sb.tile([P, 1], F32, name="total%d" % i)
            nc.vector.tensor_scalar(total[:], sums[i][:, 1:2], inv, part[:], ALU.mult, ALU.add)
            second = sb.tile([P, 1], F32, name="second%d" % i)
            nc.vector.reciprocal(second[:], total[:])
            first = sb.tile([P, 1], F32, name="first%d" % i)
            nc.vector.tensor_tensor(first[:], second[:], shifts[i][:], ALU.mult)
            factors.append((first, second))
        pieces = [(0, 256, 384), (0, 384, 512), (0, 0, 256), (1, 256, 512), (1, 0, 128), (1, 128, 256)]
        for n, (i, c0, c1) in enumerate(pieces):
            u = c0 // HALF
            res = sb.tile([P, c1 - c0], F32, name="res%d" % n)
            nc.vector.scalar_tensor_tensor(res[:], es[i][:, c0:c1], factors[i][u][:], weighted[i][:, c0:c1], ALU.mult, ALU.max)
            queue = nc.sync if n % 2 == 0 else nc.scalar
            queue.dma_start(out[i * P : (i + 1) * P, c0:c1], res[:])
